import numpy as np
import ml_dtypes


def mxq(x, axis, fmt="e4m3"):
    dtype, down = {"e4m3": (ml_dtypes.float8_e4m3fn, 7), "e5m2": (ml_dtypes.float8_e5m2, 14)}[fmt]
    v = np.moveaxis(np.asarray(x, np.float32).astype(ml_dtypes.bfloat16).astype(np.float64), axis, -1)
    blocks = v.reshape(v.shape[:-1] + (-1, 32))
    amax = np.abs(blocks).max(-1, keepdims=True)
    byte = np.maximum(np.where(amax > 0, np.frexp(amax)[1] - 1 + 127, 0) - down, 1)
    scale = np.exp2(byte - 127.0)
    codes = (blocks / scale).astype(np.float32).astype(dtype).astype(np.float64)
    return np.moveaxis((codes * scale).reshape(v.shape), -1, axis)


WIDE = False


def mx_kscale(k):
    if not WIDE:
        return np.ones(k)
    levels = np.array([10, -10, 5, -5, 0])
    if k % 512:
        return np.exp2(np.random.permutation(np.resize(levels, k // 32))).repeat(32)
    a = np.empty((k // 512, 16))
    for p in range(k // 512):
        a[p, :8] = np.random.permutation(np.resize(levels, 8))
        for g in range(8):
            far = levels[np.abs(levels - a[p, g]) >= 10]
            a[p, g + 8] = far[np.random.randint(len(far))]
    return np.exp2(a.ravel()).repeat(32)


def f64(x):
    return np.asarray(x).astype(np.float64)


def striped8(idx):
    return np.concatenate([v.reshape(-1, 16).T for v in idx]).astype(np.uint16)


def unstriped8(offs):
    return np.stack([offs[16 * g:16 * g + 16].T.reshape(-1) for g in range(8)]).astype(np.int64)


E2M1 = np.array([0.0, 0.5, 1.0, 1.5, 2.0, 3.0, 4.0, 6.0, -0.0, -0.5, -1.0, -1.5, -2.0, -3.0, -4.0, -6.0])


def pack_weight(w, fmt):
    k, n = w.shape
    w = f64(np.asarray(w, np.float32).astype(ml_dtypes.bfloat16)).reshape(k // 32, 32, n)
    amax = np.abs(w).max(1)
    if fmt == "e4m3":
        byte = np.frexp(amax)[1] - 1 + 127 - 7
    else:
        mant, ex = np.frexp(amax / 6.0)
        byte = np.where(mant > 0.5, ex, ex - 1) + 127
    byte = np.clip(np.where(amax > 0, byte, 1), 1, 254)
    scaled = (w * np.exp2(127.0 - byte)[:, None, :]).reshape(k, n).astype(np.float32)
    by_word = np.ascontiguousarray(scaled.reshape(k // 512, 128, 4, n).transpose(0, 1, 3, 2))
    if fmt == "e4m3":
        words = by_word.astype(ml_dtypes.float8_e4m3fn).view(np.uint8)
    else:
        c = by_word.astype(ml_dtypes.float4_e2m1fn).view(np.uint8) & 0xF
        words = (c[..., 0::2] | (c[..., 1::2] << 4)).reshape(k // 512, 128, 2 * n)
    return np.ascontiguousarray(words), np.ascontiguousarray(byte.astype(np.uint8).reshape(k // 512, 16, n))


def unpack_weight(words, scales, fmt):
    g, _, n = scales.shape
    words = np.ascontiguousarray(words).reshape(g, 128, n, -1)
    if fmt == "e4m3":
        vals = words.view(ml_dtypes.float8_e4m3fn).astype(np.float64)
    else:
        nib = np.empty((g, 128, n, 4), np.uint8)
        nib[..., 0::2] = words & 0xF
        nib[..., 1::2] = words >> 4
        vals = E2M1[nib]
    vals = vals * np.repeat(np.exp2(scales.astype(np.float64) - 127.0), 8, axis=1)[..., None]
    return vals.transpose(0, 1, 3, 2).reshape(g * 512, n)


K, M, T, S = 512, 512, 1024, 512


def setup_inputs():
    n = np.random.standard_normal
    s = mx_kscale(K)[:, None]
    p_w = pack_weight(n((K, M)) / np.sqrt(K) / s, "e4m3")
    return {
        "xT": (n((K, T)) * s).astype(np.float32),
        "w_words": p_w[0],
        "w_scales": p_w[1],
        "wgt": np.repeat(np.random.uniform(0.5, 2.0, (8, S)), 16, axis=0).astype(np.float32),
        "wgo": np.repeat(np.random.uniform(0.5, 2.0, (8, S)), 16, axis=0).astype(np.float32),
        "offs": striped8(np.stack([np.random.permutation(T)[:S] for _ in range(8)])),
        "offs2": striped8(np.stack([np.random.permutation(T)[:S] for _ in range(8)])),
    }


def reference(xT, w_words, w_scales, wgt, wgo, offs, offs2):
    idx = unstriped8(offs)
    group = np.arange(K) % 512 // 64
    xg = f64(wgt)[np.arange(K) // 4 % 128] * f64(xT)[np.arange(K)[:, None], idx[group]]
    xT_ = mxq(xg, 0, "e4m3")
    w_ = unpack_weight(w_words, w_scales, "e4m3")
    y = w_.T @ xT_
    place = unstriped8(offs2)[np.arange(M) % 128 // 16]
    out = np.zeros((M, T))
    out[np.arange(M)[:, None], place] = f64(wgo)[np.arange(M) % 128] * (y)
    return out

@@ -1,0 +1,131 @@
+from contextlib import ExitStack
+
+import concourse.mybir as mybir
+
+K, M, T, S = 512, 512, 1024, 512
+P = 128
+PACK = 4
+HALF = 256
+FLOPS = 2 * K * M * S
+
+F32 = mybir.dt.float32
+BF16 = mybir.dt.bfloat16
+U32 = mybir.dt.uint32
+I32 = mybir.dt.int32
+U16 = mybir.dt.uint16
+U8 = mybir.dt.uint8
+FP8X4 = mybir.dt.float8_e4m3fn_x4
+MULT = mybir.AluOpType.mult
+
+
+def tile_list_hboth_none_kernel(tc, xT, w_words, w_scales, wgt, wgo, offs, offs2, out):
+    nc = tc.nc
+    rows = M // P
+    with ExitStack() as ctx:
+        keep = ctx.enter_context(tc.tile_pool(name="keep", bufs=1))
+        psum = ctx.enter_context(tc.psum_pool(name="psum", bufs=1))
+
+        offs_sb = keep.tile([P, S // 16], U16, name="offs_sb")
+        offs2_sb = keep.tile([P, S // 16], U16, name="offs2_sb")
+        wgt_sb = keep.tile([P, S], F32, name="wgt_sb")
+        wgo_sb = keep.tile([P, S], F32, name="wgo_sb")
+        w_codes = keep.tile([P, M], U32, name="w_codes", align_bytes=64)
+        w_sc = keep.tile([P, M], U8, name="w_sc", align_bytes=64)
+        table = [keep.tile([P, T], F32, name="table%d" % i) for i in range(PACK)]
+        window = [keep.tile([P, T], F32, name="window%d" % b) for b in range(rows - 1)]
+        early = [keep.tile([P, 2, HALF], F32, name="early%d" % h) for h in range(2)]
+        grouped = [keep.tile([P, HALF, PACK], BF16, name="grouped%d" % h, align_bytes=64) for h in range(2)]
+        x_codes = [keep.tile([P, HALF], U32, name="x_codes%d" % h, align_bytes=64) for h in range(2)]
+        x_sc = [keep.tile([P, HALF], U8, name="x_sc%d" % h, align_bytes=64) for h in range(2)]
+        bank = [[psum.tile([P, HALF], F32, name="bank%d_%d" % (h, b)) for b in range(rows)] for h in range(2)]
+        y = [[keep.tile([P, HALF], F32, name="y%d_%d" % (h, b)) for b in range(rows)] for h in range(2)]
+
+        x_planes = xT.rearrange("(p i) t -> i p t", i=PACK)
+        lo, hi = slice(0, HALF), slice(HALF, S)
+        cols = [lo, hi]
+        lists = [slice(0, HALF // 16), slice(HALF // 16, S // 16)]
+
+        nc.sync.dma_start(table[0][:], x_planes[0])
+        nc.sync.dma_start(offs_sb[:], offs)
+        nc.sync.dma_start(wgt_sb[:, lo], wgt[:, lo])
+        nc.sync.dma_start(wgt_sb[:, hi], wgt[:, hi])
+        for i in range(1, PACK):
+            nc.sync.dma_start(table[i][:], x_planes[i])
+        nc.sync.dma_start(w_codes[:].bitcast(I32), w_words[0].rearrange("p n i -> p (n i)").bitcast(I32))
+        nc.sync.dma_start(offs2_sb[:], offs2)
+        nc.sync.dma_start(wgo_sb[:], wgo)
+
+        nc.vector.memset(w_sc[:].bitcast(I32), 0)
+        for q in range(4):
+            nc.gpsimd.dma_start(w_sc[32 * q : 32 * q + 4, :].bitcast(I32), w_scales[0, 4 * q : 4 * q + 4, :].bitcast(I32))
+        for b in range(rows - 1):
+            nc.vector.memset(window[b][:], 0.0)
+
+        def gather(result, h, i, first=0, last=HALF):
+            start = h * HALF
+            nc.vector.tensor_tensor(
+                result,
+                table[i][:].indirect(offs_sb[:, (start + first) // 16 : (start + last) // 16]),
+                wgt_sb[:, start + first : start + last],
+                MULT,
+            )
+
+        def interleave(h, i, source, first=0, last=HALF):
+            count = source.shape[1]
+            nc.scalar.copy(grouped[h][:, first:last, i : i + count], source.rearrange("p i n -> p n i"))
+
+        def quantize(h):
+            nc.vector.quantize_mx(
+                out=x_codes[h][:].bitcast(FP8X4), scales=x_sc[h][:], in_=grouped[h][:].rearrange("p n i -> p (n i)")
+            )
+
+        def multiply(h, b):
+            m = slice(P * b, P * b + P)
+            nc.tensor.matmul_mx(
+                out=bank[h][b][:],
+                lhsT=w_codes[:, m].bitcast(FP8X4),
+                lhsT_scale=w_sc[:, m],
+                rhs=x_codes[h][:].bitcast(FP8X4),
+                rhs_scale=x_sc[h][:],
+                start=True,
+                stop=True,
+            )
+
+        def empty(h, b):
+            nc.scalar.copy(y[h][b][:], bank[h][b][:])
+
+        def scatter(h, b):
+            nc.vector.tensor_tensor(window[b][:].indirect(offs2_sb[:, lists[h]]), y[h][b][:], wgo_sb[:, cols[h]], MULT)
+
+        for i in range(2):
+            for h in range(2):
+                gather(early[h][:, i, :], h, i)
+        for h in range(2):
+            interleave(h, 0, early[h][:])
+        late = keep.tile([P, 2, HALF], F32, name="late0")
+        gather(late[:, 0, :], 0, 2)
+        for first in range(0, HALF, P):
+            last = first + P
+            gather(late[:, 1, first:last], 0, 3, first, last)
+            interleave(0, 2, late[:, :, first:last], first, last)
+        quantize(0)
+        for b in range(rows):
+            multiply(0, b)
+            empty(0, b)
+        window.append(keep.tile([P, T], F32, name="window3", tag="table0"))
+        nc.gpsimd.memset(window[rows - 1][:], 0.0)
+        plane2 = keep.tile([P, 1, HALF], F32, name="plane2")
+        gather(plane2[:, 0, :], 1, 2)
+        interleave(1, 2, plane2[:])
+        plane3 = keep.tile([P, 1, HALF], F32, name="plane3")
+        gather(plane3[:, 0, :], 1, 3)
+        interleave(1, 3, plane3[:])
+        scatter(0, 0)
+        quantize(1)
+        for b in range(1, rows):
+            scatter(0, b)
+        for b in range(rows):
+            multiply(1, b)
+            empty(1, b)
+            scatter(1, b)
+            nc.sync.dma_start(out[P * b : P * b + P, :], window[b][:])

@@ -33,17 +33,23 @@ def tile_list_hboth_none_kernel(tc, xT, w_words, w_scales, wgt, wgo, offs, offs2
         w_sc = keep.tile([P, M], U8, name="w_sc", align_bytes=64)
         table = [keep.tile([P, T], F32, name="table%d" % i) for i in range(PACK)]
         window = [keep.tile([P, T], F32, name="window%d" % b) for b in range(rows - 1)]
+
+        chunks = [(0, P), (P, HALF), (HALF, S)]
+        widths = [last - first for first, last in chunks]
         early = [keep.tile([P, 2, HALF], F32, name="early%d" % h) for h in range(2)]
-        grouped = [keep.tile([P, HALF, PACK], BF16, name="grouped%d" % h, align_bytes=64) for h in range(2)]
-        x_codes = [keep.tile([P, HALF], U32, name="x_codes%d" % h, align_bytes=64) for h in range(2)]
-        x_sc = [keep.tile([P, HALF], U8, name="x_sc%d" % h, align_bytes=64) for h in range(2)]
-        bank = [[psum.tile([P, HALF], F32, name="bank%d_%d" % (h, b)) for b in range(rows)] for h in range(2)]
-        y = [[keep.tile([P, HALF], F32, name="y%d_%d" % (h, b)) for b in range(rows)] for h in range(2)]
+        late = [keep.tile([P, 2, n], F32, name="late%d" % c) for c, n in enumerate(widths)]
+        grouped = [keep.tile([P, n, PACK], BF16, name="grouped%d" % c, align_bytes=64) for c, n in enumerate(widths)]
+        x_codes = [keep.tile([P, n], U32, name="x_codes%d" % c, align_bytes=64) for c, n in enumerate(widths)]
+        x_sc = [keep.tile([P, n], U8, name="x_sc%d" % c, align_bytes=64) for c, n in enumerate(widths)]
+        lead_bank = psum.tile([P, P], F32, name="lead_bank")
+        next_bank = psum.tile([P, rows - 1, P], F32, name="next_bank")
+        rest_bank = [psum.tile([P, S - P], F32, name="rest_bank%d" % b) for b in range(rows)]
+        y_lead = keep.tile([P, P], F32, name="y_lead")
+        y_next = keep.tile([P, rows - 1, P], F32, name="y_next")
+        y_rest = [keep.tile([P, S - P], F32, name="y_rest%d" % b) for b in range(rows)]
 
         x_planes = xT.rearrange("(p i) t -> i p t", i=PACK)
         lo, hi = slice(0, HALF), slice(HALF, S)
-        cols = [lo, hi]
-        lists = [slice(0, HALF // 16), slice(HALF // 16, S // 16)]
 
         nc.sync.dma_start(table[0][:], x_planes[0])
         nc.sync.dma_start(offs_sb[:], offs)
@@ -61,71 +67,64 @@ def tile_list_hboth_none_kernel(tc, xT, w_words, w_scales, wgt, wgo, offs, offs2
         for b in range(rows - 1):
             nc.vector.memset(window[b][:], 0.0)
 
-        def gather(result, h, i, first=0, last=HALF):
-            start = h * HALF
+        def gather(result, i, first, last):
             nc.vector.tensor_tensor(
-                result,
-                table[i][:].indirect(offs_sb[:, (start + first) // 16 : (start + last) // 16]),
-                wgt_sb[:, start + first : start + last],
-                MULT,
+                result, table[i][:].indirect(offs_sb[:, first // 16 : last // 16]), wgt_sb[:, first:last], MULT
             )
 
-        def interleave(h, i, source, first=0, last=HALF):
-            count = source.shape[1]
-            nc.scalar.copy(grouped[h][:, first:last, i : i + count], source.rearrange("p i n -> p n i"))
+        def interleave(c, i, source):
+            nc.scalar.copy(grouped[c][:, :, i : i + 2], source.rearrange("p i n -> p n i"))
 
-        def quantize(h):
+        def quantize(c):
             nc.vector.quantize_mx(
-                out=x_codes[h][:].bitcast(FP8X4), scales=x_sc[h][:], in_=grouped[h][:].rearrange("p n i -> p (n i)")
+                out=x_codes[c][:].bitcast(FP8X4), scales=x_sc[c][:], in_=grouped[c][:].rearrange("p n i -> p (n i)")
             )
 
-        def multiply(h, b):
+        def multiply(result, c, b):
             m = slice(P * b, P * b + P)
             nc.tensor.matmul_mx(
-                out=bank[h][b][:],
+                out=result,
                 lhsT=w_codes[:, m].bitcast(FP8X4),
                 lhsT_scale=w_sc[:, m],
-                rhs=x_codes[h][:].bitcast(FP8X4),
-                rhs_scale=x_sc[h][:],
+                rhs=x_codes[c][:].bitcast(FP8X4),
+                rhs_scale=x_sc[c][:],
                 start=True,
                 stop=True,
             )
 
-        def empty(h, b):
-            nc.scalar.copy(y[h][b][:], bank[h][b][:])
-
-        def scatter(h, b):
-            nc.vector.tensor_tensor(window[b][:].indirect(offs2_sb[:, lists[h]]), y[h][b][:], wgo_sb[:, cols[h]], MULT)
+        def scatter(b, source, first, last):
+            nc.vector.tensor_tensor(
+                window[b][:].indirect(offs2_sb[:, first // 16 : last // 16]), source, wgo_sb[:, first:last], MULT
+            )
 
         for i in range(2):
             for h in range(2):
-                gather(early[h][:, i, :], h, i)
-        for h in range(2):
-            interleave(h, 0, early[h][:])
-        late = keep.tile([P, 2, HALF], F32, name="late0")
-        gather(late[:, 0, :], 0, 2)
-        for first in range(0, HALF, P):
-            last = first + P
-            gather(late[:, 1, first:last], 0, 3, first, last)
-            interleave(0, 2, late[:, :, first:last], first, last)
-        quantize(0)
-        for b in range(rows):
-            multiply(0, b)
-            empty(0, b)
+                gather(early[h][:, i, :], i, h * HALF, h * HALF + HALF)
+        interleave(0, 0, early[0][:, :, 0:P])
+        interleave(1, 0, early[0][:, :, P:HALF])
+        interleave(2, 0, early[1][:])
         window.append(keep.tile([P, T], F32, name="window3", tag="table0"))
         nc.gpsimd.memset(window[rows - 1][:], 0.0)
-        plane2 = keep.tile([P, 1, HALF], F32, name="plane2")
-        gather(plane2[:, 0, :], 1, 2)
-        interleave(1, 2, plane2[:])
-        plane3 = keep.tile([P, 1, HALF], F32, name="plane3")
-        gather(plane3[:, 0, :], 1, 3)
-        interleave(1, 3, plane3[:])
-        scatter(0, 0)
-        quantize(1)
+        for c, (first, last) in enumerate(chunks):
+            gather(late[c][:, 0, :], 2, first, last)
+        gather(late[0][:, 1, :], 3, 0, P)
+        interleave(0, 2, late[0][:])
+        quantize(0)
+        multiply(lead_bank[:], 0, 0)
+        nc.vector.tensor_copy(y_lead[:], lead_bank[:])
+        scatter(0, y_lead[:], 0, P)
         for b in range(1, rows):
-            scatter(0, b)
+            multiply(next_bank[:, b - 1, :], 0, b)
+        nc.scalar.copy(y_next[:], next_bank[:])
+        for c in (1, 2):
+            gather(late[c][:, 1, :], 3, *chunks[c])
+            interleave(c, 2, late[c][:])
+            quantize(c)
+        for b in range(1, rows):
+            scatter(b, y_next[:, b - 1, :], 0, P)
         for b in range(rows):
-            multiply(1, b)
-            empty(1, b)
-            scatter(1, b)
+            multiply(rest_bank[b][:, 0:P], 1, b)
+            multiply(rest_bank[b][:, P : S - P], 2, b)
+            nc.scalar.copy(y_rest[b][:], rest_bank[b][:])
+            scatter(b, y_rest[b][:], P, S)
             nc.sync.dma_start(out[P * b : P * b + P, :], window[b][:])

@@ -27,25 +27,24 @@ def tile_list_hboth_none_kernel(tc, xT, w_words, w_scales, wgt, wgo, offs, offs2
 
         offs_sb = keep.tile([P, S // 16], U16, name="offs_sb")
         offs2_sb = keep.tile([P, S // 16], U16, name="offs2_sb")
-        wgt_sb = keep.tile([P, S], F32, name="wgt_sb")
+        shared = keep.tile([P, 7, P], F32, name="shared")
+        wgt_sb = shared[:, 0:4, :].rearrange("p c n -> p (c n)")
         wgo_sb = keep.tile([P, S], F32, name="wgo_sb")
         w_codes = keep.tile([P, M], U32, name="w_codes", align_bytes=64)
         w_sc = keep.tile([P, M], U8, name="w_sc", align_bytes=64)
         table = [keep.tile([P, T], F32, name="table%d" % i) for i in range(PACK)]
         window = [keep.tile([P, T], F32, name="window%d" % b) for b in range(rows - 1)]
 
-        chunks = [(0, P), (P, HALF), (HALF, S)]
-        widths = [last - first for first, last in chunks]
+        chunks = S // P
         early = [keep.tile([P, 2, HALF], F32, name="early%d" % h) for h in range(2)]
-        late = [keep.tile([P, 2, n], F32, name="late%d" % c) for c, n in enumerate(widths)]
-        grouped = [keep.tile([P, n, PACK], BF16, name="grouped%d" % c, align_bytes=64) for c, n in enumerate(widths)]
-        x_codes = [keep.tile([P, n], U32, name="x_codes%d" % c, align_bytes=64) for c, n in enumerate(widths)]
-        x_sc = [keep.tile([P, n], U8, name="x_sc%d" % c, align_bytes=64) for c, n in enumerate(widths)]
+        middle = keep.tile([P, 2, P], F32, name="middle")
+        grouped = [keep.tile([P, P, PACK], BF16, name="grouped%d" % c, align_bytes=64) for c in range(chunks)]
+        x_codes = [keep.tile([P, P], U32, name="x_codes%d" % c, align_bytes=64) for c in range(chunks)]
+        x_sc = [keep.tile([P, P], U8, name="x_sc%d" % c, align_bytes=64) for c in range(chunks)]
         lead_bank = psum.tile([P, P], F32, name="lead_bank")
         next_bank = psum.tile([P, rows - 1, P], F32, name="next_bank")
-        rest_bank = [psum.tile([P, S - P], F32, name="rest_bank%d" % b) for b in range(rows)]
+        rest_bank = [psum.tile([P, chunks - 1, P], F32, name="rest_bank%d" % b) for b in range(rows)]
         y_lead = keep.tile([P, P], F32, name="y_lead")
-        y_next = keep.tile([P, rows - 1, P], F32, name="y_next")
         y_rest = [keep.tile([P, S - P], F32, name="y_rest%d" % b) for b in range(rows)]
 
         x_planes = xT.rearrange("(p i) t -> i p t", i=PACK)
@@ -100,31 +99,38 @@ def tile_list_hboth_none_kernel(tc, xT, w_words, w_scales, wgt, wgo, offs, offs2
         for i in range(2):
             for h in range(2):
                 gather(early[h][:, i, :], i, h * HALF, h * HALF + HALF)
-        interleave(0, 0, early[0][:, :, 0:P])
-        interleave(1, 0, early[0][:, :, P:HALF])
-        interleave(2, 0, early[1][:])
+        for c in range(chunks):
+            interleave(c, 0, early[c // 2][:, :, c % 2 * P : c % 2 * P + P])
         window.append(keep.tile([P, T], F32, name="window3", tag="table0"))
         nc.gpsimd.memset(window[rows - 1][:], 0.0)
-        for c, (first, last) in enumerate(chunks):
-            gather(late[c][:, 0, :], 2, first, last)
-        gather(late[0][:, 1, :], 3, 0, P)
-        interleave(0, 2, late[0][:])
+        gather(shared[:, 5, :], 2, 0, P)
+        gather(middle[:, 0, :], 2, P, 2 * P)
+        gather(shared[:, 4, :], 2, 2 * P, 3 * P)
+        gather(shared[:, 6, :], 3, 0, P)
+        interleave(0, 2, shared[:, 5:7, :])
+        gather(middle[:, 1, :], 3, P, 2 * P)
+        gather(shared[:, 0, :], 2, 3 * P, S)
         quantize(0)
         multiply(lead_bank[:], 0, 0)
-        nc.vector.tensor_copy(y_lead[:], lead_bank[:])
-        scatter(0, y_lead[:], 0, P)
+        nc.scalar.copy(y_lead[:], lead_bank[:])
         for b in range(1, rows):
             multiply(next_bank[:, b - 1, :], 0, b)
+        interleave(1, 2, middle[:])
+        gather(shared[:, 5, :], 3, 2 * P, 3 * P)
+        gather(shared[:, 6, :], 3, 3 * P, S)
+        interleave(2, 2, shared[:, 4:6, :])
+        quantize(1)
+        nc.vector.tensor_copy(grouped[3][:, :, 2:4], shared[:, 0:7:6, :].rearrange("p i n -> p n i"))
+        quantize(2)
+        quantize(3)
+        scatter(0, y_lead[:], 0, P)
+        y_next = keep.tile([P, rows - 1, P], F32, name="y_next", tag="shared")
         nc.scalar.copy(y_next[:], next_bank[:])
-        for c in (1, 2):
-            gather(late[c][:, 1, :], 3, *chunks[c])
-            interleave(c, 2, late[c][:])
-            quantize(c)
         for b in range(1, rows):
             scatter(b, y_next[:, b - 1, :], 0, P)
         for b in range(rows):
-            multiply(rest_bank[b][:, 0:P], 1, b)
-            multiply(rest_bank[b][:, P : S - P], 2, b)
-            nc.scalar.copy(y_rest[b][:], rest_bank[b][:])
+            for c in range(1, chunks):
+                multiply(rest_bank[b][:, c - 1, :], c, b)
+            nc.scalar.copy(y_rest[b][:], rest_bank[b][:].rearrange("p c n -> p (c n)"))
             scatter(b, y_rest[b][:], P, S)
             nc.sync.dma_start(out[P * b : P * b + P, :], window[b][:])

@@ -27,48 +27,66 @@ def tile_list_hboth_none_kernel(tc, xT, w_words, w_scales, wgt, wgo, offs, offs2
 
         offs_sb = keep.tile([P, S // 16], U16, name="offs_sb")
         offs2_sb = keep.tile([P, S // 16], U16, name="offs2_sb")
-        shared = keep.tile([P, 7, P], F32, name="shared")
-        wgt_sb = shared[:, 0:4, :].rearrange("p c n -> p (c n)")
+        REST = S - P
+        picked = keep.tile([P, PACK, REST], F32, name="picked", align_bytes=64)
+        wgt_lead = picked[:, 2, 0:P]
+        wgt_rest = keep.tile([P, REST], F32, name="wgt_rest", align_bytes=64)
+        lead = picked[:].rearrange("p i n -> p (i n)")[:, 3 * REST - P : 3 * REST + P].rearrange("p (i n) -> p i n", i=2)
         wgo_sb = keep.tile([P, S], F32, name="wgo_sb")
         w_codes = keep.tile([P, M], U32, name="w_codes", align_bytes=64)
         w_sc = keep.tile([P, M], U8, name="w_sc", align_bytes=64)
         table = [keep.tile([P, T], F32, name="table%d" % i) for i in range(PACK)]
-        window = [keep.tile([P, T], F32, name="window%d" % b) for b in range(rows - 1)]
+        window = [keep.tile([P, T], F32, name="window%d" % b) for b in range(1)]
 
-        chunks = S // P
-        early = [keep.tile([P, 2, HALF], F32, name="early%d" % h) for h in range(2)]
-        middle = keep.tile([P, 2, P], F32, name="middle")
-        grouped = [keep.tile([P, P, PACK], BF16, name="grouped%d" % c, align_bytes=64) for c in range(chunks)]
-        x_codes = [keep.tile([P, P], U32, name="x_codes%d" % c, align_bytes=64) for c in range(chunks)]
-        x_sc = [keep.tile([P, P], U8, name="x_sc%d" % c, align_bytes=64) for c in range(chunks)]
-        lead_bank = psum.tile([P, P], F32, name="lead_bank")
-        next_bank = psum.tile([P, rows - 1, P], F32, name="next_bank")
-        rest_bank = [psum.tile([P, chunks - 1, P], F32, name="rest_bank%d" % b) for b in range(rows)]
-        y_lead = keep.tile([P, P], F32, name="y_lead")
-        y_rest = [keep.tile([P, S - P], F32, name="y_rest%d" % b) for b in range(rows)]
+        widths = [P, P, HALF]
+        early = keep.tile([P, 2, P], F32, name="early")
+        grouped = [keep.tile([P, P, PACK], BF16, name="grouped0", align_bytes=64)]
+        x_codes = [keep.tile([P, n], U32, name="x_codes%d" % c, align_bytes=64) for c, n in enumerate(widths)]
+        x_sc = [keep.tile([P, n], U8, name="x_sc%d" % c, align_bytes=64) for c, n in enumerate(widths)]
+        lead_bank = [psum.tile([P, P], F32, name="lead_bank%d" % b) for b in range(2)]
+        pair_bank = psum.tile([P, 2, P], F32, name="pair_bank")
+        middle_bank = psum.tile([P, P], F32, name="middle_bank")
+        rest_bank = [psum.tile([P, REST], F32, name="rest_bank%d" % b) for b in range(rows)]
+        y_lead = [keep.tile([P, P], F32, name="y_lead%d" % b) for b in range(2)]
+        y_middle = keep.tile([P, P], F32, name="y_middle")
+        y_rest = [keep.tile([P, REST], F32, name="y_rest%d" % b) for b in range(rows)]
 
         x_planes = xT.rearrange("(p i) t -> i p t", i=PACK)
-        lo, hi = slice(0, HALF), slice(HALF, S)
 
+        wgt_rows = keep.tile([P, 32], F32, name="wgt_rows", align_bytes=64)
+        wgt_turned = keep.tile([P, 32], F32, name="wgt_turned", align_bytes=64)
+        wgt_spread = keep.tile([P, 16, 2, 16], F32, name="wgt_spread", align_bytes=64)
+        nc.sync.dma_start(wgt_rows[:], wgt.rearrange("p (h n) -> (p h) n", h=2)[0 : 2 * P : 17, :].rearrange("m (b x) -> m b x", x=32))
         nc.sync.dma_start(table[0][:], x_planes[0])
         nc.sync.dma_start(offs_sb[:], offs)
-        nc.sync.dma_start(wgt_sb[:, lo], wgt[:, lo])
-        nc.sync.dma_start(wgt_sb[:, hi], wgt[:, hi])
         for i in range(1, PACK):
             nc.sync.dma_start(table[i][:], x_planes[i])
         nc.sync.dma_start(w_codes[:].bitcast(I32), w_words[0].rearrange("p n i -> p (n i)").bitcast(I32))
-        nc.sync.dma_start(offs2_sb[:], offs2)
-        nc.sync.dma_start(wgo_sb[:], wgo)
-
         nc.vector.memset(w_sc[:].bitcast(I32), 0)
         for q in range(4):
-            nc.gpsimd.dma_start(w_sc[32 * q : 32 * q + 4, :].bitcast(I32), w_scales[0, 4 * q : 4 * q + 4, :].bitcast(I32))
-        for b in range(rows - 1):
-            nc.vector.memset(window[b][:], 0.0)
+            nc.sync.dma_start(w_sc[32 * q : 32 * q + 4, :].bitcast(I32), w_scales[0, 4 * q : 4 * q + 4, :].bitcast(I32))
+        nc.sync.dma_start(offs2_sb[:], offs2)
+        nc.sync.dma_start(wgo_sb[:], wgo)
+        nc.vector.memset(window[0][:], 0.0)
+
+        nc.vector.transpose(wgt_turned[:], wgt_rows[:])
+        turned = wgt_turned[:].rearrange("p (h b) -> p b h", h=2)
+        for b in (slice(0, 4), slice(4, 16)):
+            count = b.stop - b.start
+            nc.vector.tensor_copy(wgt_spread[:, b, :, :], turned[:, b, :].unsqueeze(3).to_broadcast([P, count, 2, 16]))
+        spread = wgt_spread[:].rearrange("p b h r -> p (b h r)")
+        nc.vector.transpose(wgt_lead, spread[:, 0:P])
+        nc.vector.transpose(wgt_rest[:, 0:P], spread[:, P:HALF])
+        nc.vector.transpose(wgt_rest[:, P:REST], spread[:, HALF:S])
 
         def gather(result, i, first, last):
-            nc.vector.tensor_tensor(
-                result, table[i][:].indirect(offs_sb[:, first // 16 : last // 16]), wgt_sb[:, first:last], MULT
+            weights = wgt_lead if first == 0 else wgt_rest[:, first - P : last - P]
+            nc.vector.tensor_tensor(result, table[i][:].indirect(offs_sb[:, first // 16 : last // 16]), weights, MULT)
+
+        def weave(c, first, last):
+            nc.scalar.copy(
+                grouped[c][:, :, :].rearrange("p (c n) i -> p c i n", n=4),
+                picked[:, :, first - P : last - P].rearrange("p i (c n) -> p c i n", n=4),
             )
 
         def interleave(c, i, source):
@@ -76,7 +94,7 @@ def tile_list_hboth_none_kernel(tc, xT, w_words, w_scales, wgt, wgo, offs, offs2
 
         def quantize(c):
             nc.vector.quantize_mx(
-                out=x_codes[c][:].bitcast(FP8X4), scales=x_sc[c][:], in_=grouped[c][:].rearrange("p n i -> p (n i)")
+                out=x_codes[c][:].bitcast(FP8X4), scales=x_sc[c][:], in_=grouped[c][:, :, :].rearrange("p n i -> p (n i)")
             )
 
         def multiply(result, c, b):
@@ -97,40 +115,46 @@ def tile_list_hboth_none_kernel(tc, xT, w_words, w_scales, wgt, wgo, offs, offs2
             )
 
         for i in range(2):
-            for h in range(2):
-                gather(early[h][:, i, :], i, h * HALF, h * HALF + HALF)
-        for c in range(chunks):
-            interleave(c, 0, early[c // 2][:, :, c % 2 * P : c % 2 * P + P])
-        window.append(keep.tile([P, T], F32, name="window3", tag="table0"))
-        nc.gpsimd.memset(window[rows - 1][:], 0.0)
-        gather(shared[:, 5, :], 2, 0, P)
-        gather(middle[:, 0, :], 2, P, 2 * P)
-        gather(shared[:, 4, :], 2, 2 * P, 3 * P)
-        gather(shared[:, 6, :], 3, 0, P)
-        interleave(0, 2, shared[:, 5:7, :])
-        gather(middle[:, 1, :], 3, P, 2 * P)
-        gather(shared[:, 0, :], 2, 3 * P, S)
+            gather(early[:, i, :], i, 0, P)
+            gather(picked[:, i, :], i, P, S)
+        interleave(0, 0, early[:])
+        window.append(keep.tile([P, T], F32, name="window1", tag="wgt_spread", align_bytes=64))
+        nc.gpsimd.memset(window[1][:], 0.0)
+        for i in range(2):
+            window.append(keep.tile([P, T], F32, name="window%d" % (2 + i), tag="table%d" % i))
+            nc.gpsimd.memset(window[2 + i][:], 0.0)
+        for i in range(2):
+            gather(lead[:, i, :], 2 + i, 0, P)
+        interleave(0, 2, lead)
+        gather(picked[:, 2, 0:HALF], 2, P, P + HALF)
         quantize(0)
-        multiply(lead_bank[:], 0, 0)
-        nc.scalar.copy(y_lead[:], lead_bank[:])
-        for b in range(1, rows):
-            multiply(next_bank[:, b - 1, :], 0, b)
-        interleave(1, 2, middle[:])
-        gather(shared[:, 5, :], 3, 2 * P, 3 * P)
-        gather(shared[:, 6, :], 3, 3 * P, S)
-        interleave(2, 2, shared[:, 4:6, :])
-        quantize(1)
-        nc.vector.tensor_copy(grouped[3][:, :, 2:4], shared[:, 0:7:6, :].rearrange("p i n -> p n i"))
-        quantize(2)
-        quantize(3)
-        scatter(0, y_lead[:], 0, P)
-        y_next = keep.tile([P, rows - 1, P], F32, name="y_next", tag="shared")
-        nc.scalar.copy(y_next[:], next_bank[:])
-        for b in range(1, rows):
-            scatter(b, y_next[:, b - 1, :], 0, P)
-        for b in range(rows):
-            for c in range(1, chunks):
-                multiply(rest_bank[b][:, c - 1, :], c, b)
-            nc.scalar.copy(y_rest[b][:], rest_bank[b][:].rearrange("p c n -> p (c n)"))
-            scatter(b, y_rest[b][:], P, S)
+        for b in range(2):
+            multiply(lead_bank[b][:], 0, b)
+            nc.scalar.copy(y_lead[b][:], lead_bank[b][:])
+        for b in range(2):
+            multiply(pair_bank[:, b, :], 0, 2 + b)
+        gather(picked[:, 2, HALF:REST], 2, P + HALF, S)
+        gather(picked[:, 3, :], 3, P, S)
+        for b in range(2):
+            scatter(b, y_lead[b][:], 0, P)
+        grouped_rest = keep.tile([P, REST, PACK], BF16, name="grouped_rest", tag="x_codes0", align_bytes=64)
+        grouped.extend([grouped_rest[:, 0:P, :], grouped_rest[:, P:REST, :]])
+        y_third = keep.tile([P, P], F32, name="y_third", tag="x_sc0", align_bytes=64)
+        y_pair = [y_third[:], picked[:, 0, P:HALF]]
+        bounds = [0, P, HALF, S]
+        for c in (1, 2):
+            weave(c, bounds[c], bounds[c + 1])
+            quantize(c)
+            nc.scalar.copy(y_pair[c - 1], pair_bank[:, c - 1, :])
+            scatter(1 + c, y_pair[c - 1], 0, P)
+        multiply(middle_bank[:], 1, 0)
+        nc.scalar.copy(y_middle[:], middle_bank[:])
+        scatter(0, y_middle[:], P, HALF)
+        for b in (1, 2, 3, 0):
+            first = HALF if b == 0 else P
+            if b > 0:
+                multiply(rest_bank[b][:, 0:P], 1, b)
+            multiply(rest_bank[b][:, P:REST], 2, b)
+            nc.scalar.copy(y_rest[b][:, first - P : REST], rest_bank[b][:, first - P : REST])
+            scatter(b, y_rest[b][:, first - P : REST], first, S)
             nc.sync.dma_start(out[P * b : P * b + P, :], window[b][:])

@@ -36,7 +36,7 @@ def tile_list_hboth_none_kernel(tc, xT, w_words, w_scales, wgt, wgo, offs, offs2
         w_codes = keep.tile([P, M], U32, name="w_codes", align_bytes=64)
         w_sc = keep.tile([P, M], U8, name="w_sc", align_bytes=64)
         table = [keep.tile([P, T], F32, name="table%d" % i) for i in range(PACK)]
-        window = [keep.tile([P, T], F32, name="window%d" % b) for b in range(1)]
+        window = [keep.tile([P, T], F32, name="window%d" % b) for b in range(rows - 1)]
 
         widths = [P, P, HALF]
         early = keep.tile([P, 2, P], F32, name="early")
@@ -67,7 +67,8 @@ def tile_list_hboth_none_kernel(tc, xT, w_words, w_scales, wgt, wgo, offs, offs2
             nc.sync.dma_start(w_sc[32 * q : 32 * q + 4, :].bitcast(I32), w_scales[0, 4 * q : 4 * q + 4, :].bitcast(I32))
         nc.sync.dma_start(offs2_sb[:], offs2)
         nc.sync.dma_start(wgo_sb[:], wgo)
-        nc.vector.memset(window[0][:], 0.0)
+        for b in range(rows - 1):
+            nc.vector.memset(window[b][:], 0.0)
 
         nc.vector.transpose(wgt_turned[:], wgt_rows[:])
         turned = wgt_turned[:].rearrange("p (h b) -> p b h", h=2)
@@ -118,11 +119,8 @@ def tile_list_hboth_none_kernel(tc, xT, w_words, w_scales, wgt, wgo, offs, offs2
             gather(early[:, i, :], i, 0, P)
             gather(picked[:, i, :], i, P, S)
         interleave(0, 0, early[:])
-        window.append(keep.tile([P, T], F32, name="window1", tag="wgt_spread", align_bytes=64))
-        nc.gpsimd.memset(window[1][:], 0.0)
-        for i in range(2):
-            window.append(keep.tile([P, T], F32, name="window%d" % (2 + i), tag="table%d" % i))
-            nc.gpsimd.memset(window[2 + i][:], 0.0)
+        window.append(keep.tile([P, T], F32, name="window3", tag="table0"))
+        nc.gpsimd.memset(window[rows - 1][:], 0.0)
         for i in range(2):
             gather(lead[:, i, :], 2 + i, 0, P)
         interleave(0, 2, lead)

@@ -20,75 +20,63 @@ MULT = mybir.AluOpType.mult
 
 def tile_list_hboth_none_kernel(tc, xT, w_words, w_scales, wgt, wgo, offs, offs2, out):
     nc = tc.nc
-    rows = M // P
     with ExitStack() as ctx:
         keep = ctx.enter_context(tc.tile_pool(name="keep", bufs=1))
         psum = ctx.enter_context(tc.psum_pool(name="psum", bufs=1))
 
+        LEAD, MID = P, 3 * P
         offs_sb = keep.tile([P, S // 16], U16, name="offs_sb")
         offs2_sb = keep.tile([P, S // 16], U16, name="offs2_sb")
-        REST = S - P
-        picked = keep.tile([P, PACK, REST], F32, name="picked", align_bytes=64)
-        wgt_lead = picked[:, 2, 0:P]
-        wgt_rest = keep.tile([P, REST], F32, name="wgt_rest", align_bytes=64)
-        lead = picked[:].rearrange("p i n -> p (i n)")[:, 3 * REST - P : 3 * REST + P].rearrange("p (i n) -> p i n", i=2)
+        wgt_sb = keep.tile([P, S], F32, name="wgt_sb", align_bytes=64)
         wgo_sb = keep.tile([P, S], F32, name="wgo_sb")
         w_codes = keep.tile([P, M], U32, name="w_codes", align_bytes=64)
         w_sc = keep.tile([P, M], U8, name="w_sc", align_bytes=64)
         table = [keep.tile([P, T], F32, name="table%d" % i) for i in range(PACK)]
-        window = [keep.tile([P, T], F32, name="window%d" % b) for b in range(rows - 1)]
+        staged = keep.tile([P, 26 * P], F32, name="staged")
+        plane2, plane0, last0, lead3, plane1, middle3 = 0, 3 * P, 6 * P, 8 * P + P // 2, 10 * P, 13 * P
 
-        widths = [P, P, HALF]
-        early = keep.tile([P, 2, P], F32, name="early")
-        grouped = [keep.tile([P, P, PACK], BF16, name="grouped0", align_bytes=64)]
-        x_codes = [keep.tile([P, n], U32, name="x_codes%d" % c, align_bytes=64) for c, n in enumerate(widths)]
+        def run(start, count):
+            return staged[:, start : start + count]
+
+        def pair(start, other, count):
+            step = other - start
+            return staged[:, start : start + 2 * step].rearrange("p (i n) -> p i n", i=2)[:, :, 0:count]
+        widths = [LEAD, MID - LEAD, S - MID]
+        grouped = [keep.tile([P, widths[c], PACK], BF16, name="grouped%d" % c, align_bytes=64) for c in range(2)]
+        x_codes = [keep.tile([P, widths[c]], U32, name="x_codes%d" % c, align_bytes=64) for c in range(2)]
         x_sc = [keep.tile([P, n], U8, name="x_sc%d" % c, align_bytes=64) for c, n in enumerate(widths)]
-        lead_bank = [psum.tile([P, P], F32, name="lead_bank%d" % b) for b in range(2)]
-        pair_bank = psum.tile([P, 2, P], F32, name="pair_bank")
-        middle_bank = psum.tile([P, P], F32, name="middle_bank")
-        rest_bank = [psum.tile([P, REST], F32, name="rest_bank%d" % b) for b in range(rows)]
-        y_lead = [keep.tile([P, P], F32, name="y_lead%d" % b) for b in range(2)]
-        y_middle = keep.tile([P, P], F32, name="y_middle")
-        y_rest = [keep.tile([P, REST], F32, name="y_rest%d" % b) for b in range(rows)]
-
-        x_planes = xT.rearrange("(p i) t -> i p t", i=PACK)
-
         wgt_rows = keep.tile([P, 32], F32, name="wgt_rows", align_bytes=64)
         wgt_turned = keep.tile([P, 32], F32, name="wgt_turned", align_bytes=64)
         wgt_spread = keep.tile([P, 16, 2, 16], F32, name="wgt_spread", align_bytes=64)
+        window = [keep.tile([P, T], F32, name="window0")]
+
+        x_planes = xT.rearrange("(p i) t -> i p t", i=PACK)
         nc.sync.dma_start(wgt_rows[:], wgt.rearrange("p (h n) -> (p h) n", h=2)[0 : 2 * P : 17, :].rearrange("m (b x) -> m b x", x=32))
         nc.sync.dma_start(table[0][:], x_planes[0])
         nc.sync.dma_start(offs_sb[:], offs)
         for i in range(1, PACK):
             nc.sync.dma_start(table[i][:], x_planes[i])
+        nc.sync.dma_start(wgo_sb[:, 0:LEAD], wgo[:, 0:LEAD])
         nc.sync.dma_start(w_codes[:].bitcast(I32), w_words[0].rearrange("p n i -> p (n i)").bitcast(I32))
+        nc.sync.dma_start(offs2_sb[:], offs2)
         nc.vector.memset(w_sc[:].bitcast(I32), 0)
         for q in range(4):
             nc.sync.dma_start(w_sc[32 * q : 32 * q + 4, :].bitcast(I32), w_scales[0, 4 * q : 4 * q + 4, :].bitcast(I32))
-        nc.sync.dma_start(offs2_sb[:], offs2)
-        nc.sync.dma_start(wgo_sb[:], wgo)
-        for b in range(rows - 1):
-            nc.vector.memset(window[b][:], 0.0)
+        nc.sync.dma_start(wgo_sb[:, LEAD:S], wgo[:, LEAD:S])
+        nc.vector.memset(window[0][:], 0.0)
+        window3 = keep.tile([P, T], F32, name="window3")
+        nc.vector.memset(window3[:], 0.0)
 
         nc.vector.transpose(wgt_turned[:], wgt_rows[:])
         turned = wgt_turned[:].rearrange("p (h b) -> p b h", h=2)
         for b in (slice(0, 4), slice(4, 16)):
-            count = b.stop - b.start
-            nc.vector.tensor_copy(wgt_spread[:, b, :, :], turned[:, b, :].unsqueeze(3).to_broadcast([P, count, 2, 16]))
+            nc.vector.tensor_copy(wgt_spread[:, b, :, :], turned[:, b, :].unsqueeze(3).to_broadcast([P, b.stop - b.start, 2, 16]))
         spread = wgt_spread[:].rearrange("p b h r -> p (b h r)")
-        nc.vector.transpose(wgt_lead, spread[:, 0:P])
-        nc.vector.transpose(wgt_rest[:, 0:P], spread[:, P:HALF])
-        nc.vector.transpose(wgt_rest[:, P:REST], spread[:, HALF:S])
+        for n in (slice(0, LEAD), slice(LEAD, MID), slice(MID, S)):
+            nc.vector.transpose(wgt_sb[:, n], spread[:, n])
 
         def gather(result, i, first, last):
-            weights = wgt_lead if first == 0 else wgt_rest[:, first - P : last - P]
-            nc.vector.tensor_tensor(result, table[i][:].indirect(offs_sb[:, first // 16 : last // 16]), weights, MULT)
-
-        def weave(c, first, last):
-            nc.scalar.copy(
-                grouped[c][:, :, :].rearrange("p (c n) i -> p c i n", n=4),
-                picked[:, :, first - P : last - P].rearrange("p i (c n) -> p c i n", n=4),
-            )
+            nc.vector.tensor_tensor(result, table[i][:].indirect(offs_sb[:, first // 16 : last // 16]), wgt_sb[:, first:last], MULT)
 
         def interleave(c, i, source):
             nc.scalar.copy(grouped[c][:, :, i : i + 2], source.rearrange("p i n -> p n i"))
@@ -110,49 +98,57 @@ def tile_list_hboth_none_kernel(tc, xT, w_words, w_scales, wgt, wgo, offs, offs2
                 stop=True,
             )
 
-        def scatter(b, source, first, last):
-            nc.vector.tensor_tensor(
-                window[b][:].indirect(offs2_sb[:, first // 16 : last // 16]), source, wgo_sb[:, first:last], MULT
-            )
+        pieces = [(0, 0, LEAD), (1, 0, LEAD), (2, 0, MID), (3, 0, S), (2, MID, S), (0, LEAD, S), (1, LEAD, S)]
+        bank = [psum.tile([P, last - first], F32, name="bank%d" % n) for n, (b, first, last) in enumerate(pieces)]
+        y = [keep.tile([P, last - first], F32, name="y%d" % n, align_bytes=64) for n, (b, first, last) in enumerate(pieces)]
+        bounds = [0, LEAD, MID, S]
 
-        for i in range(2):
-            gather(early[:, i, :], i, 0, P)
-            gather(picked[:, i, :], i, P, S)
-        interleave(0, 0, early[:])
-        window.append(keep.tile([P, T], F32, name="window3", tag="table0"))
-        nc.gpsimd.memset(window[rows - 1][:], 0.0)
-        for i in range(2):
-            gather(lead[:, i, :], 2 + i, 0, P)
-        interleave(0, 2, lead)
-        gather(picked[:, 2, 0:HALF], 2, P, P + HALF)
+        def products(c):
+            for n, (b, first, last) in enumerate(pieces):
+                if first <= bounds[c] and bounds[c + 1] <= last:
+                    multiply(bank[n][:, bounds[c] - first : bounds[c + 1] - first], c, b)
+
+        def place(n):
+            b, first, last = pieces[n]
+            nc.scalar.copy(y[n][:], bank[n][:])
+            nc.vector.tensor_tensor(window[b][:].indirect(offs2_sb[:, first // 16 : last // 16]), y[n][:], wgo_sb[:, first:last], MULT)
+            if last == S:
+                nc.sync.dma_start(out[P * b : P * b + P, :], window[b][:])
+
+        window.append(keep.tile([P, T], F32, name="window1", tag="wgt_spread", align_bytes=64))
+        nc.gpsimd.memset(window[1][:], 0.0)
+        gather(run(plane0, LEAD), 0, 0, LEAD)
+        gather(run(plane0 + LEAD, S - LEAD), 0, LEAD, S)
+        window.append(keep.tile([P, T], F32, name="window2", tag="table0"))
+        nc.gpsimd.memset(window[2][:], 0.0)
+        window.append(window3)
+        gather(run(plane1, MID), 1, 0, MID)
+        gather(run(last0 + P, P), 1, MID, S)
+        interleave(0, 0, pair(plane0, plane1, LEAD))
+        interleave(1, 0, pair(plane0 + LEAD, plane1 + LEAD, MID - LEAD))
+        gather(run(plane2, MID), 2, 0, MID)
+        gather(run(lead3, LEAD), 3, 0, LEAD)
+        interleave(0, 2, pair(plane2, lead3, LEAD))
+        for h in range(2):
+            gather(run(middle3 + h * P, P), 3, LEAD + h * P, LEAD + h * P + P)
+            nc.scalar.copy(
+                grouped[1][:, h * P : h * P + P, 2:4], pair(plane2 + LEAD + h * P, middle3 + h * P, P).rearrange("p i n -> p n i")
+            )
         quantize(0)
-        for b in range(2):
-            multiply(lead_bank[b][:], 0, b)
-            nc.scalar.copy(y_lead[b][:], lead_bank[b][:])
-        for b in range(2):
-            multiply(pair_bank[:, b, :], 0, 2 + b)
-        gather(picked[:, 2, HALF:REST], 2, P + HALF, S)
-        gather(picked[:, 3, :], 3, P, S)
-        for b in range(2):
-            scatter(b, y_lead[b][:], 0, P)
-        grouped_rest = keep.tile([P, REST, PACK], BF16, name="grouped_rest", tag="x_codes0", align_bytes=64)
-        grouped.extend([grouped_rest[:, 0:P, :], grouped_rest[:, P:REST, :]])
-        y_third = keep.tile([P, P], F32, name="y_third", tag="x_sc0", align_bytes=64)
-        y_pair = [y_third[:], picked[:, 0, P:HALF]]
-        bounds = [0, P, HALF, S]
-        for c in (1, 2):
-            weave(c, bounds[c], bounds[c + 1])
-            quantize(c)
-            nc.scalar.copy(y_pair[c - 1], pair_bank[:, c - 1, :])
-            scatter(1 + c, y_pair[c - 1], 0, P)
-        multiply(middle_bank[:], 1, 0)
-        nc.scalar.copy(y_middle[:], middle_bank[:])
-        scatter(0, y_middle[:], P, HALF)
-        for b in (1, 2, 3, 0):
-            first = HALF if b == 0 else P
-            if b > 0:
-                multiply(rest_bank[b][:, 0:P], 1, b)
-            multiply(rest_bank[b][:, P:REST], 2, b)
-            nc.scalar.copy(y_rest[b][:, first - P : REST], rest_bank[b][:, first - P : REST])
-            scatter(b, y_rest[b][:, first - P : REST], first, S)
-            nc.sync.dma_start(out[P * b : P * b + P, :], window[b][:])
+        products(0)
+        for i in (2, 3):
+            gather(run(last0 + i * P, P), i, MID, S)
+        quantize(1)
+        place(0)
+        place(1)
+        products(1)
+        grouped.append(keep.tile([P, S - MID, PACK], BF16, name="grouped2", tag="x_codes0", align_bytes=64))
+        nc.scalar.copy(
+            grouped[2][:, :, :].rearrange("p (c n) i -> p c i n", n=4), run(last0, PACK * P).rearrange("p (i c n) -> p c i n", i=PACK, n=4)
+        )
+        x_codes.append(keep.tile([P, widths[2]], U32, name="x_codes2", align_bytes=64))
+        quantize(2)
+        place(2)
+        products(2)
+        for n in range(3, len(pieces)):
+            place(n)

@@ -56,12 +56,12 @@ def tile_list_hboth_none_kernel(tc, xT, w_words, w_scales, wgt, wgo, offs, offs2
         nc.sync.dma_start(offs_sb[:], offs)
         for i in range(1, PACK):
             nc.sync.dma_start(table[i][:], x_planes[i])
-        nc.sync.dma_start(wgo_sb[:, 0:LEAD], wgo[:, 0:LEAD])
-        nc.sync.dma_start(w_codes[:].bitcast(I32), w_words[0].rearrange("p n i -> p (n i)").bitcast(I32))
-        nc.sync.dma_start(offs2_sb[:], offs2)
         nc.vector.memset(w_sc[:].bitcast(I32), 0)
         for q in range(4):
-            nc.sync.dma_start(w_sc[32 * q : 32 * q + 4, :].bitcast(I32), w_scales[0, 4 * q : 4 * q + 4, :].bitcast(I32))
+            nc.gpsimd.dma_start(w_sc[32 * q : 32 * q + 4, :].bitcast(I32), w_scales[0, 4 * q : 4 * q + 4, :].bitcast(I32))
+        nc.sync.dma_start(w_codes[:].bitcast(I32), w_words[0].rearrange("p n i -> p (n i)").bitcast(I32))
+        nc.sync.dma_start(offs2_sb[:], offs2)
+        nc.sync.dma_start(wgo_sb[:, 0:LEAD], wgo[:, 0:LEAD])
         nc.sync.dma_start(wgo_sb[:, LEAD:S], wgo[:, LEAD:S])
         nc.vector.memset(window[0][:], 0.0)
         window3 = keep.tile([P, T], F32, name="window3")
@@ -113,7 +113,10 @@ def tile_list_hboth_none_kernel(tc, xT, w_words, w_scales, wgt, wgo, offs, offs2
             nc.scalar.copy(y[n][:], bank[n][:])
             nc.vector.tensor_tensor(window[b][:].indirect(offs2_sb[:, first // 16 : last // 16]), y[n][:], wgo_sb[:, first:last], MULT)
             if last == S:
-                nc.sync.dma_start(out[P * b : P * b + P, :], window[b][:])
+                parts = 2 if n < len(pieces) - 2 else 1
+                for h in range(parts):
+                    cols = slice(h * T // parts, (h + 1) * T // parts)
+                    nc.sync.dma_start(out[P * b : P * b + P, cols], window[b][:, cols])
 
         window.append(keep.tile([P, T], F32, name="window1", tag="wgt_spread", align_bytes=64))
         nc.gpsimd.memset(window[1][:], 0.0)

@@ -58,14 +58,13 @@ def tile_list_hboth_none_kernel(tc, xT, w_words, w_scales, wgt, wgo, offs, offs2
             nc.sync.dma_start(table[i][:], x_planes[i])
         nc.vector.memset(w_sc[:].bitcast(I32), 0)
         for q in range(4):
-            nc.gpsimd.dma_start(w_sc[32 * q : 32 * q + 4, :].bitcast(I32), w_scales[0, 4 * q : 4 * q + 4, :].bitcast(I32))
+            nc.sync.dma_start(w_sc[32 * q : 32 * q + 4, :].bitcast(I32), w_scales[0, 4 * q : 4 * q + 4, :].bitcast(I32))
         nc.sync.dma_start(w_codes[:].bitcast(I32), w_words[0].rearrange("p n i -> p (n i)").bitcast(I32))
         nc.sync.dma_start(offs2_sb[:], offs2)
-        nc.sync.dma_start(wgo_sb[:, 0:LEAD], wgo[:, 0:LEAD])
-        nc.sync.dma_start(wgo_sb[:, LEAD:S], wgo[:, LEAD:S])
+        nc.sync.dma_start(wgo_sb[:], wgo)
         nc.vector.memset(window[0][:], 0.0)
         window3 = keep.tile([P, T], F32, name="window3")
-        nc.vector.memset(window3[:], 0.0)
+        nc.gpsimd.memset(window3[:], 0.0)
 
         nc.vector.transpose(wgt_turned[:], wgt_rows[:])
         turned = wgt_turned[:].rearrange("p (h b) -> p b h", h=2)
@@ -113,10 +112,8 @@ def tile_list_hboth_none_kernel(tc, xT, w_words, w_scales, wgt, wgo, offs, offs2
             nc.scalar.copy(y[n][:], bank[n][:])
             nc.vector.tensor_tensor(window[b][:].indirect(offs2_sb[:, first // 16 : last // 16]), y[n][:], wgo_sb[:, first:last], MULT)
             if last == S:
-                parts = 2 if n < len(pieces) - 2 else 1
-                for h in range(parts):
-                    cols = slice(h * T // parts, (h + 1) * T // parts)
-                    nc.sync.dma_start(out[P * b : P * b + P, cols], window[b][:, cols])
+                queue = nc.gpsimd if n == 3 else nc.sync
+                queue.dma_start(out[P * b : P * b + P, :], window[b][:])
 
         window.append(keep.tile([P, T], F32, name="window1", tag="wgt_spread", align_bytes=64))
         nc.gpsimd.memset(window[1][:], 0.0)

@@ -112,8 +112,10 @@ def tile_list_hboth_none_kernel(tc, xT, w_words, w_scales, wgt, wgo, offs, offs2
             nc.scalar.copy(y[n][:], bank[n][:])
             nc.vector.tensor_tensor(window[b][:].indirect(offs2_sb[:, first // 16 : last // 16]), y[n][:], wgo_sb[:, first:last], MULT)
             if last == S:
-                queue = nc.gpsimd if n == 3 else nc.sync
-                queue.dma_start(out[P * b : P * b + P, :], window[b][:])
+                parts = {3: 4, 4: 4, 5: 2, 6: 1}[n]
+                for h in range(parts):
+                    cols = slice(h * T // parts, (h + 1) * T // parts)
+                    nc.sync.dma_start(out[P * b : P * b + P, cols], window[b][:, cols])
 
         window.append(keep.tile([P, T], F32, name="window1", tag="wgt_spread", align_bytes=64))
         nc.gpsimd.memset(window[1][:], 0.0)

@@ -33,7 +33,7 @@ def tile_list_hboth_none_kernel(tc, xT, w_words, w_scales, wgt, wgo, offs, offs2
         w_sc = keep.tile([P, M], U8, name="w_sc", align_bytes=64)
         table = [keep.tile([P, T], F32, name="table%d" % i) for i in range(PACK)]
         staged = keep.tile([P, 26 * P], F32, name="staged")
-        plane2, plane0, last0, lead3, plane1, middle3 = 0, 3 * P, 6 * P, 8 * P + P // 2, 10 * P, 13 * P
+        plane2, plane0, last0, lead3, plane1, middle3 = 0, 3 * P, 6 * P, 7 * P + P // 2, 10 * P, 13 * P
 
         def run(start, count):
             return staged[:, start : start + count]
@@ -125,7 +125,6 @@ def tile_list_hboth_none_kernel(tc, xT, w_words, w_scales, wgt, wgo, offs, offs2
         nc.gpsimd.memset(window[2][:], 0.0)
         window.append(window3)
         gather(run(plane1, MID), 1, 0, MID)
-        gather(run(last0 + P, P), 1, MID, S)
         interleave(0, 0, pair(plane0, plane1, LEAD))
         interleave(1, 0, pair(plane0 + LEAD, plane1 + LEAD, MID - LEAD))
         gather(run(plane2, MID), 2, 0, MID)
@@ -136,9 +135,10 @@ def tile_list_hboth_none_kernel(tc, xT, w_words, w_scales, wgt, wgo, offs, offs2
             nc.scalar.copy(
                 grouped[1][:, h * P : h * P + P, 2:4], pair(plane2 + LEAD + h * P, middle3 + h * P, P).rearrange("p i n -> p n i")
             )
+        gather(run(last0 + 3 * P, P), 3, MID, S)
         quantize(0)
         products(0)
-        for i in (2, 3):
+        for i in (1, 2):
             gather(run(last0 + i * P, P), i, MID, S)
         quantize(1)
         place(0)

@@ -5,7 +5,6 @@ import concourse.mybir as mybir
 K, M, T, S = 512, 512, 1024, 512
 P = 128
 PACK = 4
-HALF = 256
 FLOPS = 2 * K * M * S
 
 F32 = mybir.dt.float32
@@ -27,20 +26,23 @@ def tile_list_hboth_none_kernel(tc, xT, w_words, w_scales, wgt, wgo, offs, offs2
         LEAD, MID = P, 3 * P
         offs_sb = keep.tile([P, S // 16], U16, name="offs_sb")
         offs2_sb = keep.tile([P, S // 16], U16, name="offs2_sb")
-        wgt_sb = keep.tile([P, S], F32, name="wgt_sb", align_bytes=64)
         wgo_sb = keep.tile([P, S], F32, name="wgo_sb")
         w_codes = keep.tile([P, M], U32, name="w_codes", align_bytes=64)
         w_sc = keep.tile([P, M], U8, name="w_sc", align_bytes=64)
         table = [keep.tile([P, T], F32, name="table%d" % i) for i in range(PACK)]
-        staged = keep.tile([P, 26 * P], F32, name="staged")
-        plane2, plane0, last0, lead3, plane1, middle3 = 0, 3 * P, 6 * P, 7 * P + P // 2, 10 * P, 13 * P
+        staged = keep.tile([P, 22 * P], F32, name="staged", align_bytes=64)
+        cells = staged[:].rearrange("p (r n) -> p r n", n=P)
+        cell = {(0, c): 4 + c for c in range(4)}
+        cell.update({(1, c): 8 + c for c in range(4)})
+        cell.update({(3, c): 19 + c for c in range(3)})
+        cell.update({(2, 0): 15, (2, 1): 14, (2, 2): 0, (2, 3): 15, (3, 3): 19})
 
-        def run(start, count):
-            return staged[:, start : start + count]
+        def pair(i, c, count):
+            first, second = cell[i, c] * P, cell[i + 1, c] * P
+            if count == P:
+                return cells[:, cell[i, c] : cell[i + 1, c] + 1 : cell[i + 1, c] - cell[i, c], :]
+            return staged[:, first : 2 * second - first].rearrange("p (i n) -> p i n", i=2)[:, :, 0:count]
 
-        def pair(start, other, count):
-            step = other - start
-            return staged[:, start : start + 2 * step].rearrange("p (i n) -> p i n", i=2)[:, :, 0:count]
         widths = [LEAD, MID - LEAD, S - MID]
         grouped = [keep.tile([P, widths[c], PACK], BF16, name="grouped%d" % c, align_bytes=64) for c in range(2)]
         x_codes = [keep.tile([P, widths[c]], U32, name="x_codes%d" % c, align_bytes=64) for c in range(2)]
@@ -54,7 +56,7 @@ def tile_list_hboth_none_kernel(tc, xT, w_words, w_scales, wgt, wgo, offs, offs2
         nc.sync.dma_start(wgt_rows[:], wgt.rearrange("p (h n) -> (p h) n", h=2)[0 : 2 * P : 17, :].rearrange("m (b x) -> m b x", x=32))
         nc.sync.dma_start(table[0][:], x_planes[0])
         nc.sync.dma_start(offs_sb[:], offs)
-        for i in range(1, PACK):
+        for i in (1, 3, 2):
             nc.sync.dma_start(table[i][:], x_planes[i])
         nc.vector.memset(w_sc[:].bitcast(I32), 0)
         for q in range(4):
@@ -72,13 +74,13 @@ def tile_list_hboth_none_kernel(tc, xT, w_words, w_scales, wgt, wgo, offs, offs2
             nc.vector.tensor_copy(wgt_spread[:, b, :, :], turned[:, b, :].unsqueeze(3).to_broadcast([P, b.stop - b.start, 2, 16]))
         spread = wgt_spread[:].rearrange("p b h r -> p (b h r)")
         for n in (slice(0, LEAD), slice(LEAD, MID), slice(MID, S)):
-            nc.vector.transpose(wgt_sb[:, n], spread[:, n])
+            nc.vector.transpose(staged[:, n], spread[:, n])
 
-        def gather(result, i, first, last):
-            nc.vector.tensor_tensor(result, table[i][:].indirect(offs_sb[:, first // 16 : last // 16]), wgt_sb[:, first:last], MULT)
-
-        def interleave(c, i, source):
-            nc.scalar.copy(grouped[c][:, :, i : i + 2], source.rearrange("p i n -> p n i"))
+        def gather(i, first, last):
+            start = cell[i, first // P] * P
+            nc.vector.tensor_tensor(
+                staged[:, start : start + last - first], table[i][:].indirect(offs_sb[:, first // 16 : last // 16]), staged[:, first:last], MULT
+            )
 
         def quantize(c):
             nc.vector.quantize_mx(
@@ -119,34 +121,34 @@ def tile_list_hboth_none_kernel(tc, xT, w_words, w_scales, wgt, wgo, offs, offs2
 
         window.append(keep.tile([P, T], F32, name="window1", tag="wgt_spread", align_bytes=64))
         nc.gpsimd.memset(window[1][:], 0.0)
-        gather(run(plane0, LEAD), 0, 0, LEAD)
-        gather(run(plane0 + LEAD, S - LEAD), 0, LEAD, S)
+        gather(0, 0, LEAD)
+        gather(0, LEAD, S)
         window.append(keep.tile([P, T], F32, name="window2", tag="table0"))
         nc.gpsimd.memset(window[2][:], 0.0)
         window.append(window3)
-        gather(run(plane1, MID), 1, 0, MID)
-        interleave(0, 0, pair(plane0, plane1, LEAD))
-        interleave(1, 0, pair(plane0 + LEAD, plane1 + LEAD, MID - LEAD))
-        gather(run(plane2, MID), 2, 0, MID)
-        gather(run(lead3, LEAD), 3, 0, LEAD)
-        interleave(0, 2, pair(plane2, lead3, LEAD))
-        for h in range(2):
-            gather(run(middle3 + h * P, P), 3, LEAD + h * P, LEAD + h * P + P)
-            nc.scalar.copy(
-                grouped[1][:, h * P : h * P + P, 2:4], pair(plane2 + LEAD + h * P, middle3 + h * P, P).rearrange("p i n -> p n i")
-            )
-        gather(run(last0 + 3 * P, P), 3, MID, S)
+        gather(1, 0, S)
+        nc.scalar.copy(grouped[0][:, :, 0:2], pair(0, 0, P).rearrange("p i n -> p n i"))
+        nc.scalar.copy(grouped[1][:, :, 0:2], pair(0, 1, 2 * P).rearrange("p i n -> p n i"))
+        gather(3, 0, MID)
+        gather(2, 0, LEAD)
+        lead_pair = pair(2, 0, P).rearrange("p i n -> p n i")
+        nc.scalar.copy(grouped[0][:, 0:64, 2:4], lead_pair[:, 0:64, :])
+        gather(2, P, 2 * P)
+        nc.vector.tensor_copy(grouped[0][:, 64:P, 2:4], lead_pair[:, 64:P, :])
+        nc.scalar.copy(grouped[1][:, 0:P, 2:4], pair(2, 1, P).rearrange("p i n -> p n i"))
+        gather(2, 2 * P, MID)
+        nc.scalar.copy(grouped[1][:, P : 2 * P, 2:4], pair(2, 2, P).rearrange("p i n -> p n i"))
         quantize(0)
         products(0)
-        for i in (1, 2):
-            gather(run(last0 + i * P, P), i, MID, S)
+        for i in (2, 3):
+            gather(i, MID, S)
         quantize(1)
         place(0)
         place(1)
         products(1)
         grouped.append(keep.tile([P, S - MID, PACK], BF16, name="grouped2", tag="x_codes0", align_bytes=64))
         nc.scalar.copy(
-            grouped[2][:, :, :].rearrange("p (c n) i -> p c i n", n=4), run(last0, PACK * P).rearrange("p (i c n) -> p c i n", i=PACK, n=4)
+            grouped[2][:, :, :].rearrange("p (c n) i -> p c i n", n=4), cells[:, 7:20:4, :].rearrange("p i (c n) -> p c i n", n=4)
         )
         x_codes.append(keep.tile([P, widths[2]], U32, name="x_codes2", align_bytes=64))
         quantize(2)

@@ -63,7 +63,8 @@ def tile_list_hboth_none_kernel(tc, xT, w_words, w_scales, wgt, wgo, offs, offs2
             nc.sync.dma_start(w_sc[32 * q : 32 * q + 4, :].bitcast(I32), w_scales[0, 4 * q : 4 * q + 4, :].bitcast(I32))
         nc.sync.dma_start(w_codes[:].bitcast(I32), w_words[0].rearrange("p n i -> p (n i)").bitcast(I32))
         nc.sync.dma_start(offs2_sb[:], offs2)
-        nc.sync.dma_start(wgo_sb[:], wgo)
+        nc.sync.dma_start(wgo_sb[:, 0:LEAD], wgo[:, 0:LEAD])
+        nc.sync.dma_start(wgo_sb[:, LEAD:S], wgo[:, LEAD:S])
         nc.vector.memset(window[0][:], 0.0)
         window3 = keep.tile([P, T], F32, name="window3")
         nc.gpsimd.memset(window3[:], 0.0)
@@ -82,39 +83,43 @@ def tile_list_hboth_none_kernel(tc, xT, w_words, w_scales, wgt, wgo, offs, offs2
                 staged[:, start : start + last - first], table[i][:].indirect(offs_sb[:, first // 16 : last // 16]), staged[:, first:last], MULT
             )
 
-        def quantize(c):
+        def quantize(c, n=slice(None)):
             nc.vector.quantize_mx(
-                out=x_codes[c][:].bitcast(FP8X4), scales=x_sc[c][:], in_=grouped[c][:, :, :].rearrange("p n i -> p (n i)")
+                out=x_codes[c][:, n].bitcast(FP8X4), scales=x_sc[c][:, n], in_=grouped[c][:, n, :].rearrange("p n i -> p (n i)")
             )
 
-        def multiply(result, c, b):
+        def multiply(result, c, b, n=slice(None)):
             m = slice(P * b, P * b + P)
             nc.tensor.matmul_mx(
                 out=result,
                 lhsT=w_codes[:, m].bitcast(FP8X4),
                 lhsT_scale=w_sc[:, m],
-                rhs=x_codes[c][:].bitcast(FP8X4),
-                rhs_scale=x_sc[c][:],
+                rhs=x_codes[c][:, n].bitcast(FP8X4),
+                rhs_scale=x_sc[c][:, n],
                 start=True,
                 stop=True,
             )
 
         pieces = [(0, 0, LEAD), (1, 0, LEAD), (2, 0, MID), (3, 0, S), (2, MID, S), (0, LEAD, S), (1, LEAD, S)]
-        bank = [psum.tile([P, last - first], F32, name="bank%d" % n) for n, (b, first, last) in enumerate(pieces)]
+        HALF = LEAD // 2
+        halves = [slice(0, HALF), slice(HALF, LEAD)]
+        half_bank = [psum.tile([P, HALF], F32, name="half_bank%d" % h) for h in range(2)]
+        bank = {n: psum.tile([P, last - first], F32, name="bank%d" % n) for n, (b, first, last) in enumerate(pieces) if n > 0}
         y = [keep.tile([P, last - first], F32, name="y%d" % n, align_bytes=64) for n, (b, first, last) in enumerate(pieces)]
         bounds = [0, LEAD, MID, S]
 
         def products(c):
             for n, (b, first, last) in enumerate(pieces):
-                if first <= bounds[c] and bounds[c + 1] <= last:
+                if n > 0 and first <= bounds[c] and bounds[c + 1] <= last:
                     multiply(bank[n][:, bounds[c] - first : bounds[c + 1] - first], c, b)
 
         def place(n):
             b, first, last = pieces[n]
-            nc.scalar.copy(y[n][:], bank[n][:])
+            if n > 0:
+                nc.scalar.copy(y[n][:], bank[n][:])
             nc.vector.tensor_tensor(window[b][:].indirect(offs2_sb[:, first // 16 : last // 16]), y[n][:], wgo_sb[:, first:last], MULT)
             if last == S:
-                parts = {3: 4, 4: 4, 5: 2, 6: 1}[n]
+                parts = {3: 4, 4: 4, 5: 1, 6: 1}[n]
                 for h in range(parts):
                     cols = slice(h * T // parts, (h + 1) * T // parts)
                     nc.sync.dma_start(out[P * b : P * b + P, cols], window[b][:, cols])
@@ -138,11 +143,15 @@ def tile_list_hboth_none_kernel(tc, xT, w_words, w_scales, wgt, wgo, offs, offs2
         nc.scalar.copy(grouped[1][:, 0:P, 2:4], pair(2, 1, P).rearrange("p i n -> p n i"))
         gather(2, 2 * P, MID)
         nc.scalar.copy(grouped[1][:, P : 2 * P, 2:4], pair(2, 2, P).rearrange("p i n -> p n i"))
-        quantize(0)
+        for h in range(2):
+            quantize(0, halves[h])
+            multiply(half_bank[h][:], 0, 0, halves[h])
+            nc.scalar.copy(y[0][:, halves[h]], half_bank[h][:])
         products(0)
         for i in (2, 3):
             gather(i, MID, S)
-        quantize(1)
+        quantize(1, slice(0, P))
+        quantize(1, slice(P, 2 * P))
         place(0)
         place(1)
         products(1)

@@ -71,10 +71,10 @@ def tile_list_hboth_none_kernel(tc, xT, w_words, w_scales, wgt, wgo, offs, offs2
 
         nc.vector.transpose(wgt_turned[:], wgt_rows[:])
         turned = wgt_turned[:].rearrange("p (h b) -> p b h", h=2)
-        for b in (slice(0, 4), slice(4, 16)):
+        for b in (slice(0, 4), slice(4, 8), slice(8, 16)):
             nc.vector.tensor_copy(wgt_spread[:, b, :, :], turned[:, b, :].unsqueeze(3).to_broadcast([P, b.stop - b.start, 2, 16]))
         spread = wgt_spread[:].rearrange("p b h r -> p (b h r)")
-        for n in (slice(0, LEAD), slice(LEAD, MID), slice(MID, S)):
+        for n in (slice(0, LEAD), slice(LEAD, 2 * LEAD), slice(2 * LEAD, S)):
             nc.vector.transpose(staged[:, n], spread[:, n])
 
         def gather(i, first, last):
@@ -137,9 +137,10 @@ def tile_list_hboth_none_kernel(tc, xT, w_words, w_scales, wgt, wgo, offs, offs2
         gather(3, 0, MID)
         gather(2, 0, LEAD)
         lead_pair = pair(2, 0, P).rearrange("p i n -> p n i")
-        nc.scalar.copy(grouped[0][:, 0:64, 2:4], lead_pair[:, 0:64, :])
+        for n in (slice(0, 64), slice(64, 96)):
+            nc.scalar.copy(grouped[0][:, n, 2:4], lead_pair[:, n, :])
         gather(2, P, 2 * P)
-        nc.vector.tensor_copy(grouped[0][:, 64:P, 2:4], lead_pair[:, 64:P, :])
+        nc.vector.tensor_copy(grouped[0][:, 96:P, 2:4], lead_pair[:, 96:P, :])
         nc.scalar.copy(grouped[1][:, 0:P, 2:4], pair(2, 1, P).rearrange("p i n -> p n i"))
         gather(2, 2 * P, MID)
         nc.scalar.copy(grouped[1][:, P : 2 * P, 2:4], pair(2, 2, P).rearrange("p i n -> p n i"))
@@ -150,8 +151,7 @@ def tile_list_hboth_none_kernel(tc, xT, w_words, w_scales, wgt, wgo, offs, offs2
         products(0)
         for i in (2, 3):
             gather(i, MID, S)
-        quantize(1, slice(0, P))
-        quantize(1, slice(P, 2 * P))
+        quantize(1)
         place(0)
         place(1)
         products(1)

@@ -66,8 +66,6 @@ def tile_list_hboth_none_kernel(tc, xT, w_words, w_scales, wgt, wgo, offs, offs2
         nc.sync.dma_start(wgo_sb[:, 0:LEAD], wgo[:, 0:LEAD])
         nc.sync.dma_start(wgo_sb[:, LEAD:S], wgo[:, LEAD:S])
         nc.vector.memset(window[0][:], 0.0)
-        window3 = keep.tile([P, T], F32, name="window3")
-        nc.gpsimd.memset(window3[:], 0.0)
 
         nc.vector.transpose(wgt_turned[:], wgt_rows[:])
         turned = wgt_turned[:].rearrange("p (h b) -> p b h", h=2)
@@ -100,7 +98,7 @@ def tile_list_hboth_none_kernel(tc, xT, w_words, w_scales, wgt, wgo, offs, offs2
                 stop=True,
             )
 
-        pieces = [(0, 0, LEAD), (1, 0, LEAD), (2, 0, MID), (3, 0, S), (2, MID, S), (0, LEAD, S), (1, LEAD, S)]
+        pieces = [(0, 0, LEAD), (1, 0, LEAD), (2, 0, MID), (0, LEAD, S), (2, MID, S), (1, LEAD, S), (3, 0, S)]
         HALF = LEAD // 2
         halves = [slice(0, HALF), slice(HALF, LEAD)]
         half_bank = [psum.tile([P, HALF], F32, name="half_bank%d" % h) for h in range(2)]
@@ -130,7 +128,6 @@ def tile_list_hboth_none_kernel(tc, xT, w_words, w_scales, wgt, wgo, offs, offs2
         gather(0, LEAD, S)
         window.append(keep.tile([P, T], F32, name="window2", tag="table0"))
         nc.gpsimd.memset(window[2][:], 0.0)
-        window.append(window3)
         gather(1, 0, S)
         nc.scalar.copy(grouped[0][:, :, 0:2], pair(0, 0, P).rearrange("p i n -> p n i"))
         nc.scalar.copy(grouped[1][:, :, 0:2], pair(0, 1, 2 * P).rearrange("p i n -> p n i"))
@@ -151,7 +148,8 @@ def tile_list_hboth_none_kernel(tc, xT, w_words, w_scales, wgt, wgo, offs, offs2
         products(0)
         for i in (2, 3):
             gather(i, MID, S)
-        quantize(1)
+        quantize(1, slice(0, P))
+        quantize(1, slice(P, 2 * P))
         place(0)
         place(1)
         products(1)
@@ -161,6 +159,8 @@ def tile_list_hboth_none_kernel(tc, xT, w_words, w_scales, wgt, wgo, offs, offs2
         )
         x_codes.append(keep.tile([P, widths[2]], U32, name="x_codes2", align_bytes=64))
         quantize(2)
+        window.append(keep.tile([P, T], F32, name="window3", tag="x_codes0", align_bytes=64))
+        nc.gpsimd.memset(window[3][:], 0.0)
         place(2)
         products(2)
         for n in range(3, len(pieces)):

@@ -48,7 +48,7 @@ def tile_list_hboth_none_kernel(tc, xT, w_words, w_scales, wgt, wgo, offs, offs2
         x_codes = [keep.tile([P, widths[c]], U32, name="x_codes%d" % c, align_bytes=64) for c in range(2)]
         x_sc = [keep.tile([P, n], U8, name="x_sc%d" % c, align_bytes=64) for c, n in enumerate(widths)]
         wgt_rows = keep.tile([P, 32], F32, name="wgt_rows", align_bytes=64)
-        wgt_turned = keep.tile([P, 32], F32, name="wgt_turned", align_bytes=64)
+        wgt_turned = staged[:, cell[0, 0] * P : cell[0, 0] * P + 32]
         wgt_spread = keep.tile([P, 16, 2, 16], F32, name="wgt_spread", align_bytes=64)
         window = [keep.tile([P, T], F32, name="window0")]
 
@@ -67,10 +67,10 @@ def tile_list_hboth_none_kernel(tc, xT, w_words, w_scales, wgt, wgo, offs, offs2
         nc.sync.dma_start(wgo_sb[:, LEAD:S], wgo[:, LEAD:S])
         nc.vector.memset(window[0][:], 0.0)
 
-        nc.vector.transpose(wgt_turned[:], wgt_rows[:])
-        turned = wgt_turned[:].rearrange("p (h b) -> p b h", h=2)
-        for b in (slice(0, 4), slice(4, 8), slice(8, 16)):
-            nc.vector.tensor_copy(wgt_spread[:, b, :, :], turned[:, b, :].unsqueeze(3).to_broadcast([P, b.stop - b.start, 2, 16]))
+        nc.vector.transpose(wgt_turned, wgt_rows[:])
+        turned = wgt_turned.rearrange("p (h b) -> p b h", h=2)
+        for copy, b in ((nc.vector.tensor_copy, slice(0, 4)), (nc.vector.tensor_copy, slice(4, 8)), (nc.scalar.copy, slice(8, 16))):
+            copy(wgt_spread[:, b, :, :], turned[:, b, :].unsqueeze(3).to_broadcast([P, b.stop - b.start, 2, 16]))
         spread = wgt_spread[:].rearrange("p b h r -> p (b h r)")
         for n in (slice(0, LEAD), slice(LEAD, 2 * LEAD), slice(2 * LEAD, S)):
             nc.vector.transpose(staged[:, n], spread[:, n])

@@ -134,10 +134,10 @@ def tile_list_hboth_none_kernel(tc, xT, w_words, w_scales, wgt, wgo, offs, offs2
         gather(3, 0, MID)
         gather(2, 0, LEAD)
         lead_pair = pair(2, 0, P).rearrange("p i n -> p n i")
-        for n in (slice(0, 64), slice(64, 96)):
+        for n in (slice(32, 64), slice(64, P)):
             nc.scalar.copy(grouped[0][:, n, 2:4], lead_pair[:, n, :])
         gather(2, P, 2 * P)
-        nc.vector.tensor_copy(grouped[0][:, 96:P, 2:4], lead_pair[:, 96:P, :])
+        nc.vector.tensor_copy(grouped[0][:, 0:32, 2:4], lead_pair[:, 0:32, :])
         nc.scalar.copy(grouped[1][:, 0:P, 2:4], pair(2, 1, P).rearrange("p i n -> p n i"))
         gather(2, 2 * P, MID)
         nc.scalar.copy(grouped[1][:, P : 2 * P, 2:4], pair(2, 2, P).rearrange("p i n -> p n i"))

from contextlib import ExitStack

import concourse.mybir as mybir

K, M, T, S = 512, 512, 1024, 512
P = 128
PACK = 4
FLOPS = 2 * K * M * S

F32 = mybir.dt.float32
BF16 = mybir.dt.bfloat16
U32 = mybir.dt.uint32
I32 = mybir.dt.int32
U16 = mybir.dt.uint16
U8 = mybir.dt.uint8
FP8X4 = mybir.dt.float8_e4m3fn_x4
MULT = mybir.AluOpType.mult


def tile_list_hboth_none_kernel(tc, xT, w_words, w_scales, wgt, wgo, offs, offs2, out):
    nc = tc.nc
    with ExitStack() as ctx:
        keep = ctx.enter_context(tc.tile_pool(name="keep", bufs=1))
        psum = ctx.enter_context(tc.psum_pool(name="psum", bufs=1))

        LEAD, MID = P, 3 * P
        offs_sb = keep.tile([P, S // 16], U16, name="offs_sb")
        offs2_sb = keep.tile([P, S // 16], U16, name="offs2_sb")
        wgo_sb = keep.tile([P, S], F32, name="wgo_sb")
        w_codes = keep.tile([P, M], U32, name="w_codes", align_bytes=64)
        w_sc = keep.tile([P, M], U8, name="w_sc", align_bytes=64)
        table = [keep.tile([P, T], F32, name="table%d" % i) for i in range(PACK)]
        staged = keep.tile([P, 22 * P], F32, name="staged", align_bytes=64)
        cells = staged[:].rearrange("p (r n) -> p r n", n=P)
        cell = {(0, c): 4 + c for c in range(4)}
        cell.update({(1, c): 8 + c for c in range(4)})
        cell.update({(3, c): 19 + c for c in range(3)})
        cell.update({(2, 0): 15, (2, 1): 14, (2, 2): 0, (2, 3): 15, (3, 3): 19})

        def pair(i, c, count):
            first, second = cell[i, c] * P, cell[i + 1, c] * P
            if count == P:
                return cells[:, cell[i, c] : cell[i + 1, c] + 1 : cell[i + 1, c] - cell[i, c], :]
            return staged[:, first : 2 * second - first].rearrange("p (i n) -> p i n", i=2)[:, :, 0:count]

        widths = [LEAD, MID - LEAD, S - MID]
        grouped = [keep.tile([P, widths[c], PACK], BF16, name="grouped%d" % c, align_bytes=64) for c in range(2)]
        x_codes = [keep.tile([P, widths[c]], U32, name="x_codes%d" % c, align_bytes=64) for c in range(2)]
        x_sc = [keep.tile([P, n], U8, name="x_sc%d" % c, align_bytes=64) for c, n in enumerate(widths)]
        wgt_rows = keep.tile([P, 32], F32, name="wgt_rows", align_bytes=64)
        wgt_turned = staged[:, cell[0, 0] * P : cell[0, 0] * P + 32]
        wgt_spread = keep.tile([P, 16, 2, 16], F32, name="wgt_spread", align_bytes=64)
        window = [keep.tile([P, T], F32, name="window0")]

        x_planes = xT.rearrange("(p i) t -> i p t", i=PACK)
        nc.sync.dma_start(wgt_rows[:], wgt.rearrange("p (h n) -> (p h) n", h=2)[0 : 2 * P : 17, :].rearrange("m (b x) -> m b x", x=32))
        nc.sync.dma_start(table[0][:], x_planes[0])
        nc.sync.dma_start(offs_sb[:], offs)
        for i in (1, 3, 2):
            nc.sync.dma_start(table[i][:], x_planes[i])
        nc.vector.memset(w_sc[:].bitcast(I32), 0)
        for q in range(4):
            nc.sync.dma_start(w_sc[32 * q : 32 * q + 4, :].bitcast(I32), w_scales[0, 4 * q : 4 * q + 4, :].bitcast(I32))
        nc.sync.dma_start(w_codes[:].bitcast(I32), w_words[0].rearrange("p n i -> p (n i)").bitcast(I32))
        nc.sync.dma_start(offs2_sb[:], offs2)
        nc.sync.dma_start(wgo_sb[:, 0:LEAD], wgo[:, 0:LEAD])
        nc.sync.dma_start(wgo_sb[:, LEAD:S], wgo[:, LEAD:S])
        nc.vector.memset(window[0][:], 0.0)

        nc.vector.transpose(wgt_turned, wgt_rows[:])
        turned = wgt_turned.rearrange("p (h b) -> p b h", h=2)
        for copy, b in ((nc.vector.tensor_copy, slice(0, 4)), (nc.vector.tensor_copy, slice(4, 8)), (nc.scalar.copy, slice(8, 16))):
            copy(wgt_spread[:, b, :, :], turned[:, b, :].unsqueeze(3).to_broadcast([P, b.stop - b.start, 2, 16]))
        spread = wgt_spread[:].rearrange("p b h r -> p (b h r)")
        for n in (slice(0, LEAD), slice(LEAD, 2 * LEAD), slice(2 * LEAD, S)):
            nc.vector.transpose(staged[:, n], spread[:, n])

        def gather(i, first, last):
            start = cell[i, first // P] * P
            nc.vector.tensor_tensor(
                staged[:, start : start + last - first], table[i][:].indirect(offs_sb[:, first // 16 : last // 16]), staged[:, first:last], MULT
            )

        def quantize(c, n=slice(None)):
            nc.vector.quantize_mx(
                out=x_codes[c][:, n].bitcast(FP8X4), scales=x_sc[c][:, n], in_=grouped[c][:, n, :].rearrange("p n i -> p (n i)")
            )

        def multiply(result, c, b, n=slice(None)):
            m = slice(P * b, P * b + P)
            nc.tensor.matmul_mx(
                out=result,
                lhsT=w_codes[:, m].bitcast(FP8X4),
                lhsT_scale=w_sc[:, m],
                rhs=x_codes[c][:, n].bitcast(FP8X4),
                rhs_scale=x_sc[c][:, n],
                start=True,
                stop=True,
            )

        pieces = [(0, 0, LEAD), (1, 0, LEAD), (2, 0, MID), (0, LEAD, S), (2, MID, S), (1, LEAD, S), (3, 0, S)]
        HALF = LEAD // 2
        halves = [slice(0, HALF), slice(HALF, LEAD)]
        half_bank = [psum.tile([P, HALF], F32, name="half_bank%d" % h) for h in range(2)]
        bank = {n: psum.tile([P, last - first], F32, name="bank%d" % n) for n, (b, first, last) in enumerate(pieces) if n > 0}
        y = [keep.tile([P, last - first], F32, name="y%d" % n, align_bytes=64) for n, (b, first, last) in enumerate(pieces)]
        bounds = [0, LEAD, MID, S]

        def products(c):
            for n, (b, first, last) in enumerate(pieces):
                if n > 0 and first <= bounds[c] and bounds[c + 1] <= last:
                    multiply(bank[n][:, bounds[c] - first : bounds[c + 1] - first], c, b)

        def place(n):
            b, first, last = pieces[n]
            if n > 0:
                nc.scalar.copy(y[n][:], bank[n][:])
            nc.vector.tensor_tensor(window[b][:].indirect(offs2_sb[:, first // 16 : last // 16]), y[n][:], wgo_sb[:, first:last], MULT)
            if last == S:
                parts = {3: 4, 4: 4, 5: 1, 6: 1}[n]
                for h in range(parts):
                    cols = slice(h * T // parts, (h + 1) * T // parts)
                    nc.sync.dma_start(out[P * b : P * b + P, cols], window[b][:, cols])

        window.append(keep.tile([P, T], F32, name="window1", tag="wgt_spread", align_bytes=64))
        nc.gpsimd.memset(window[1][:], 0.0)
        gather(0, 0, LEAD)
        gather(0, LEAD, S)
        window.append(keep.tile([P, T], F32, name="window2", tag="table0"))
        nc.gpsimd.memset(window[2][:], 0.0)
        gather(1, 0, S)
        nc.scalar.copy(grouped[0][:, :, 0:2], pair(0, 0, P).rearrange("p i n -> p n i"))
        nc.scalar.copy(grouped[1][:, :, 0:2], pair(0, 1, 2 * P).rearrange("p i n -> p n i"))
        gather(3, 0, MID)
        gather(2, 0, LEAD)
        lead_pair = pair(2, 0, P).rearrange("p i n -> p n i")
        for n in (slice(32, 64), slice(64, P)):
            nc.scalar.copy(grouped[0][:, n, 2:4], lead_pair[:, n, :])
        gather(2, P, 2 * P)
        nc.vector.tensor_copy(grouped[0][:, 0:32, 2:4], lead_pair[:, 0:32, :])
        nc.scalar.copy(grouped[1][:, 0:P, 2:4], pair(2, 1, P).rearrange("p i n -> p n i"))
        gather(2, 2 * P, MID)
        nc.scalar.copy(grouped[1][:, P : 2 * P, 2:4], pair(2, 2, P).rearrange("p i n -> p n i"))
        for h in range(2):
            quantize(0, halves[h])
            multiply(half_bank[h][:], 0, 0, halves[h])
            nc.scalar.copy(y[0][:, halves[h]], half_bank[h][:])
        products(0)
        for i in (2, 3):
            gather(i, MID, S)
        quantize(1, slice(0, P))
        quantize(1, slice(P, 2 * P))
        place(0)
        place(1)
        products(1)
        grouped.append(keep.tile([P, S - MID, PACK], BF16, name="grouped2", tag="x_codes0", align_bytes=64))
        nc.scalar.copy(
            grouped[2][:, :, :].rearrange("p (c n) i -> p c i n", n=4), cells[:, 7:20:4, :].rearrange("p i (c n) -> p c i n", n=4)
        )
        x_codes.append(keep.tile([P, widths[2]], U32, name="x_codes2", align_bytes=64))
        quantize(2)
        window.append(keep.tile([P, T], F32, name="window3", tag="x_codes0", align_bytes=64))
        nc.gpsimd.memset(window[3][:], 0.0)
        place(2)
        products(2)
        for n in range(3, len(pieces)):
            place(n)
